import numpy as np, ml_dtypes
CORES = [16,18,20,22]
N = 4
import mx_ref
BF = ml_dtypes.bfloat16
def gcols(t, e):
    v = np.concatenate([t.reshape(8, 16, -1, 4), np.zeros((8, 16, 1, 4), BF)], axis=2)
    return np.ascontiguousarray(np.stack([v[g][:, e[g]] for g in range(8)])).reshape(128, -1)
def tile(rs):
    return np.stack(rs, axis=2).reshape(128, -1).astype(BF)
def pick(q, e):
    c = np.concatenate([q[0].reshape(128, -1, 4), np.zeros((128, 1, 4), np.uint8)], axis=1); s = np.concatenate([q[1], np.ones((16, 1), np.uint8)], axis=1)
    return (np.ascontiguousarray(c[:, e].reshape(128, -1)), np.ascontiguousarray(s[:, e]))
def join(*qs):
    return (np.concatenate([q[0] for q in qs], axis=1), np.concatenate([q[1] for q in qs], axis=1))
def put(q, e, v):
    c, s = q[0].reshape(128, -1, 4).copy(), q[1].copy(); c[:, e] = v[0].reshape(128, -1, 4); s[:, e] = v[1]
    return (c.reshape(128, -1), s)
def pk(c, s):
    return (np.ascontiguousarray(c), mx_ref.live(s))
def emit(q):
    return q[0], q[1]
def packed(v, rng):
    q = [mx_ref.quantize(np.ascontiguousarray(v[r])) for r in range(N)]
    return np.stack([a for a, b in q]), np.stack([mx_ref.plane(b, rng) for a, b in q])
def values_of_codes():
    e, c = np.zeros((128, 128, 4), np.float32), np.zeros((128, 2, 4), np.uint8)
    e[np.arange(128), np.arange(128), 0] = 1
    c[:127, :, 0] = np.arange(256).reshape(2, 128).T[:127]
    return mx_ref.matmul(mx_ref.quantize(e.reshape(128, 512).astype(BF)), (c.reshape(128, 8), np.full((16, 2), 127, np.uint8))).T.reshape(-1).astype(np.float64)
CODE_VALUE, SCALE_VALUE = values_of_codes(), 2.0 ** (np.arange(256) - 127.0)
def decode(q):
    return (CODE_VALUE[q[0]].reshape(16, 8, -1, 4) * SCALE_VALUE[q[1]][:, None, :, None] + 0.0).reshape(128, -1).astype(np.float32)
def f(rng, *shape):
    return mx_ref.flush((rng.standard_normal(shape, dtype=np.float32) * np.exp2(rng.integers(-2, 3, shape[:-1] + (1,)))).astype(BF))
def wide(rng, *shape, cols=0):
    v = rng.standard_normal(shape, dtype=np.float32) * np.exp2(rng.integers(-12, 13, shape)).astype(np.float32)
    if cols: v *= np.repeat(np.exp2(rng.integers(-cols, cols + 1, shape[:-2] + (1, shape[-1] // 4))) * (rng.random(shape[:-2] + (1, shape[-1] // 4)) > 0.0625), 4, axis=-1).astype(np.float32)
    return mx_ref.flush(v.astype(BF))
C, M, R = 448, 192, 3
def meet(n):
    i = np.arange(n)
    q = np.stack([i] * 4 + [n - 1 - i] * 4)
    for h in range(1, 8):
        k = n // 2 if h < 4 else n // 2 - 1
        q[h, [h - 1, k]] = q[h, [k, h - 1]]
    q[4, [0, 1, 2, n - 1, n - 2, n - 3]] = q[4, [n - 1, n - 2, n - 3, 0, 1, 2]]
    return q
def big(v):
    v = v.astype(np.float32)
    v[np.abs(v) < np.float32(2.0 ** -16)] = 0
    return v.astype(BF)
def numbers_of(rng):
    return {"x": big(f(rng, N, 128, 4 * C)), "u": np.array(f(rng, N, 128, 512)), "v": np.array(f(rng, N, 128, 512))}
def layers(rng, still=[]):
    w = (rng.random((N, 128, 2048)) * 2.0 - 1.0) * 0.054 * np.exp2(-rng.integers(0, 2, (N, 128, 1)))
    w = big(w).reshape(N, 8, 16, 4, 8, 16, 4)
    for i in still:
        w[:, :, i] = 0
        w[:, :, :, :, :, i] = 0
    return w
def weights(rng, w):
    c, p = packed(np.ascontiguousarray(w).reshape(N, 128, 2048), rng)
    return {"wc": c, "ws": p}
def setup_inputs(rng):
    return {**numbers_of(rng), **weights(rng, layers(rng))}
def setup_inputs_ties(rng):
    d = numbers_of(rng)
    x = d["x"].reshape(N, 8, 16, C, 4)
    x[:, :, 0] = 0
    x[:, :, 0, :, 0] = rng.integers(1, 4, (N, 8, C)).astype(np.float32).astype(BF)
    u = d["u"].reshape(N, 128, 128, 4)
    one = u[:, :, :1].copy()
    one[:, :8] = 0
    u[:, :, ::16] = 0
    o = rng.permutation(N)
    for r in range(N):
        if o[r] == 2:
            u[r, :, ::16] = one[r]
            s = mx_ref.matmul(mx_ref.quantize(np.ascontiguousarray(u[r].reshape(128, 512))), mx_ref.quantize(np.ascontiguousarray(x[r].reshape(128, 4 * C))))[0]
            x[r, 0, 0] = 0
            x[r, 0, 0, np.argsort(-s, kind="stable")[C // 2], 0] = 2.0
            u[r, 0, 0, 0] = -2.0 ** 20
        else:
            for h in range(0, 128, 16): u[r, h, h, 0] = 0.0 if o[r] == 0 else -1.0 if o[r] == 1 else 1.0
    return {"x": x.reshape(N, 128, 4 * C), "u": u.reshape(N, 128, 512), "v": d["v"], **weights(rng, layers(rng, [0]))}
def setup_inputs_near(rng):
    d = numbers_of(rng)
    x = d["x"].astype(np.float32).reshape(N, 8, 16, C, 4)
    u = d["u"].reshape(N, 128, 128, 4)
    x[:, :, 0] = 0
    x[:, :, 8:] = 0
    u[:, :, ::16] = 0
    o = rng.permutation(N) % 4
    for r in range(N):
        k = 1.0 if o[r] == 0 else 2.0 ** -30
        if o[r] < 2:
            x[r, :, 0, :, 0] = rng.integers(0, 2, (8, C)) * 2.0 - 1.0
            x[r, :, 11, :, 0] = 2.0 ** -10
        if o[r] == 2:
            e = np.argsort(rng.random((8, C)), axis=1)
            x[r, :, 0, :, 0] = np.where(e < C // 16, 1.0, np.where(e < C // 8, -1.0, 0.0))
        if o[r] < 3:
            s = rng.integers(0, 16, (8, C))
            x[r, :, 8] = ((s[:, :, None] >> np.arange(4)) & 1) * np.exp2(np.arange(4) - 23.0)
        else:
            a = rng.integers(0, 4, (8, C))
            x[r, :, 10, :, 0] = np.array([1.0, 0.0, -1.0, 0.0])[a] * 2.0 ** -27
            x[r, :, 10, :, 1] = np.array([0.0, 1.125, 1.125, 0.0])[a] * 2.0 ** -27
        for h in range(0, 128, 16):
            if o[r] < 2:
                u[r, h, h, 0] = k
                u[r, h + 11, h, 0] = k
            if o[r] == 2: u[r, h, h, 0] = 1.0
            if o[r] < 3: u[r, h + 8, h] = k
            else:
                u[r, h + 10, h, 0] = 1.25 * k
                u[r, h + 10, h, 1] = 1.125 * k
    return {"x": x.reshape(N, 128, 4 * C).astype(BF), "u": u.reshape(N, 128, 512), "v": d["v"], **weights(rng, layers(rng, [0, 8, 9, 10, 11, 12, 13, 14, 15]))}
def setup_inputs_odd(rng):
    d = numbers_of(rng)
    a = (1.0 + (2 * rng.integers(0, 64, (N, 8, 2, C, 32)) + 1) * 2.0 ** -7) * np.exp2(-rng.integers(8, 15, (N, 8, 2, C, 32))) * (rng.integers(0, 2, (N, 8, 2, C, 32)) * 2.0 - 1.0)
    e = rng.integers(0, 32, (N, 8, 2, C, 1))
    np.put_along_axis(a, e, 1.96875 * (rng.integers(0, 2, (N, 8, 2, C, 1)) * 2.0 - 1.0), axis=4)
    a *= np.exp2(rng.integers(-1, 3, (N, 8, 2, C, 1)))
    d["x"] = np.ascontiguousarray(a.reshape(N, 8, 2, C, 8, 4).transpose(0, 1, 2, 4, 3, 5)).reshape(N, 128, 4 * C).astype(np.float32).astype(BF)
    return {**d, **weights(rng, layers(rng))}
def setup_inputs_ends(rng):
    d = numbers_of(rng)
    e = rng.permutation(N)
    o = e % 4
    x = (0.9 + 0.1 * rng.random((N, 8, 16, C, 4))) * 2.0 ** 30
    x[:, :, 8:] = 2.0 ** -27 * (rng.integers(0, 2, (N, 8, 8, C, 4)) * 2.0 - 1.0)
    u, v = d["u"].reshape(N, 128, 128, 4), d["v"]
    w = np.zeros((N, 8, 16, 4, 8, 16, 4), np.float32)
    for r in range(N):
        a = np.zeros((8, 16, 8, 4))
        if o[r] == 0: x[r] = -2.0 ** 30 * (0.9 + 0.1 * rng.random((8, 16, C, 4)))
        if o[r] == 1: x[r, :, :8] *= rng.integers(0, 2, (1, 1, C, 1)) * 2.0 - 1.0
        if o[r] == 2: x[r, :, :8] *= rng.integers(0, 2, (8, 8, C, 4)) * 2.0 - 1.0
        if o[r] == 3:
            q = meet(C)[rng.permutation(8)] if e[r] == 3 else np.stack([C - 1 - np.arange(C)] * 8)
            x[r, :, :8] *= rng.integers(0, 2, (8, 1, C, 1)) * 2.0 - 1.0
            x[r, :, 0] = 0
            x[r, :, 0, :, :3] = (((C - 1 - q)[:, :, None] >> np.array([0, 3, 6])) & 7) * 2.0 ** 27
            for g in range(0 if e[r] == 3 else 4, 8): a[g, 0, g, :3] = 2.0 ** 20 * np.array([1.0, 8.0, 64.0])
        if o[r] == 0: a = 2.0 ** 30 * (1.0 - 0.1 * rng.random((8, 16, 8, 4)))
        if o[r] == 1:
            a[:, :8] = 2.0 ** 30 * (1.0 - 0.1 * rng.random((8, 8, 8, 4)))
            a *= (rng.permutation(8) % 2 * 2.0 - 1.0)[None, None, :, None]
        if o[r] == 2: a[:, 8:] = 2.0 ** -30 * (rng.integers(0, 2, (8, 8, 8, 4)) * 2.0 - 1.0)
        u[r, :, ::16] = a.reshape(128, 8, 4).astype(np.float32).astype(BF)
        if o[r] == 0: w[r, :, :8, :, :, :8] = 0.0546875
        if o[r] in (1, 3): w[r, :, :8, :, :, :8] = 0.0546875 * (rng.integers(0, 2, (8, 8, 4, 8, 8, 4)) * 2.0 - 1.0)
        if o[r] == 0: v[r] = 2.0 ** 30
        if o[r] == 1: v[r] = (2.0 ** 30 * (rng.integers(0, 2, (128, 512)) * 2.0 - 1.0)).astype(np.float32).astype(BF)
        if o[r] == 2: v[r] = (2.0 ** -30 * (rng.integers(0, 2, (128, 512)) * 2.0 - 1.0)).astype(np.float32).astype(BF)
    return {"x": x.astype(np.float32).reshape(N, 128, 4 * C).astype(BF), "u": u.reshape(N, 128, 512), "v": v, **weights(rng, w.astype(BF))}
def setup_inputs_spread(rng):
    d = setup_inputs(rng)
    d["x"] = big(wide(rng, N, 128, 4 * C, cols=6))
    return d
def check_inputs(d):
    b = []
    for k, low in (("x", 2.0 ** -27), ("u", 2.0 ** -30), ("v", 2.0 ** -30)):
        a = np.abs(d[k].astype(np.float32))
        if not (np.isfinite(a).all() and ((a == 0) | (a >= low) & (a <= 2.0 ** 30)).all()): b.append("a value of " + k)
    none, least, most = [emit(mx_ref.quantize(np.full((128, 16), k, np.float32).astype(BF)))[1][0, 0] for k in (0.0, 2.0 ** -16, 2.0 ** -5)]
    for r in range(N):
        if ((d["wc"][r] == 0x7F) | (d["wc"][r] == 0xFF)).any(): b.append("wc: a code that is no number")
        s = mx_ref.live(d["ws"][r])
        if ((s != none) & ((s < least) | (s > most))).any(): b.append("ws: a scale out of range")
        if not (np.abs(decode(pk(d["wc"][r], d["ws"][r]))) < 2.0 ** -4).all(): b.append("wc, ws: a number of W that isn't below 2**-4 in size")
    return b
def reference(x, u, v, wc, ws):
    qu = [mx_ref.quantize(u[r]) for r in range(N)]
    lay = [pk(wc[r], ws[r]) for r in range(N)]
    now = [x[r] for r in range(N)]
    l, own = [None] * N, [None] * N
    for t in range(R):
        y, z = [], []
        for r in range(N):
            q = mx_ref.quantize(now[r])
            d = decode(q).astype(BF)
            s = mx_ref.matmul(qu[r], q)[::16] + np.float32(0.0)
            o = np.argsort(-s, axis=1, kind="stable")
            place = np.argsort(o, axis=1, kind="stable")
            m = np.sort(place, axis=0)
            l[r] = np.where(place <= m[3], o[:, m[4]], o[:, m[3]])
            c = np.argsort(m[0] - m[7], kind="stable")[:M]
            own[r] = l[r][:, c]
            z.append(mx_ref.quantize(gcols(d, own[r])))
            y.append(((now[r].astype(np.float32) + gcols(d, l[r]).astype(np.float32)) * np.float32(0.5)).astype(BF))
        for r in range(N):
            came = z[(r - 1 - t) % N]
            h = tile([mx_ref.matmul(pick(lay[r], np.arange(128 * b, 128 * b + 128)), came) * np.float32(0.03125) for b in range(4)])
            first = np.full((8, C), M)
            np.minimum.at(first, (np.arange(8)[:, None], own[r]), np.arange(M)[None])
            now[r] = gcols(np.concatenate([y[r], h], axis=1), np.where(first < M, C + first, np.arange(C)[None]))
    y, ol = np.zeros((N, 128, C), np.float32), np.zeros((N, 8, C), np.float32)
    oc, osc = np.zeros((N, 128, 4 * C), np.uint8), np.zeros((N, 16, C), np.uint8)
    for r in range(N):
        q = mx_ref.quantize(now[r])
        y[r] = mx_ref.matmul(mx_ref.quantize(v[r]), q)
        ol[r] = l[r]
        oc[r], osc[r] = emit(q)
    return {"y": y, "ol": ol, "oc": oc, "osc": osc}

@@ -1,0 +1,501 @@
+from concourse.mybir import dt, AluOpType, ActivationFunctionType
+
+C, M, R, NS, MS = 448, 192, 3, 28, 12
+MAGIC = 12582912.0
+QN = [128, 128, 176, 240, 304, 368, 448]
+OP = AluOpType
+AF = ActivationFunctionType
+
+SCRATCH = {}
+ALIAS = {}
+
+
+def _sb(name, n, d):
+    SCRATCH[name] = ("sbuf", [128, n], d)
+
+
+def _mx(name, n):
+    _sb("q" + name, n, "float8_e4m3fn_x4")
+    _sb("s" + name, n, "uint8")
+
+
+def _pack(buf, d, parts):
+    at = 0
+    for n, w in parts:
+        ALIAS[n] = (buf, at, w)
+        at += (w + 15) // 16 * 16
+    _sb(buf, at, d)
+
+
+def _packmx(buf, parts):
+    at = 0
+    for n, w in parts:
+        ALIAS["q" + n] = ("q" + buf, at, w)
+        ALIAS["s" + n] = ("s" + buf, at, w)
+        at += w
+    _mx(buf, at)
+
+
+for _n in ("xa", "xb", "ft", "cr", "tl"):
+    _sb(_n, 4 * C, "bfloat16")
+_sb("ut", 512, "bfloat16")
+_sb("vt", 512, "bfloat16")
+_pack("kt", "bfloat16", [(n, 512) for n in ("ctile", "fb", "sgt", "fst", "mst", "ont", "et0", "et1", "et2", "et3")])
+_pack("tb", "bfloat16", [("t%d" % b, C) for b in range(4)])
+_pack("yh", "bfloat16", [("yh%d" % b, C + M) for b in range(4)])
+_pack("ctb", "bfloat16", [("ct%d" % q, 4 * QN[q]) for q in range(7)])
+_pack("kb", "bfloat16", [("mk", C), ("rst", C), ("iotaj", C), ("bigm", M), ("kv", M), ("i16", C), ("jwm", C), ("jwf", C)])
+_packmx("k", [(n, 128) for n in ("e0", "e1", "e2", "e3", "sg", "fs", "ms", "on")])
+_packmx("c", [("c%d" % q, QN[q]) for q in range(7)])
+for _n, _w in (("u", 128), ("ux", 128), ("v", 128), ("w", 512), ("x", C), ("f", C), ("mv", 224), ("cr", C)):
+    _mx(_n, _w)
+for _t in range(R):
+    _mx("tl%d" % _t, C)
+    _mx("z%d" % _t, M)
+    _mx("a%d" % _t, M)
+for _n, _w in (("junk0", C), ("junk1", C), ("junk2", C), ("ot", C), ("la", C), ("lm", C), ("lf", C), ("ctab", C), ("cm", M), ("cf", M), ("lk", M), ("lkm", M),
+               ("lkf", M), ("rep2", M), ("eqd", M), ("df", M), ("eqo", 12 * 192), ("st", C + M), ("stm", C), ("stf", C), ("dg", 112),
+               ("mv", 896), ("m8", 112), ("lo", 112), ("hi", 112), ("gx", 56), ("gy", 56), ("gg", 224)):
+    _sb(_n, _w, "bfloat16")
+for _n in ("sm", "swf", "rep", "em", "ef", "em2", "rf", "iot512", "kca", "ka", "yo", "olf"):
+    _sb(_n, C, "float32")
+_pack("fk", "float32", [("cst", NS), ("gm", 8), ("mb", 32), ("rst8", 32), ("kc", NS), ("j448", NS), ("nt", MS)])
+_pack("fw", "float32", [("rs", NS), ("rsc", NS), ("z", NS), ("x1", NS), ("kw", NS), ("km", 32), ("kf", 32), ("aa", 112), ("bb", 112), ("a2", 56), ("b2", 56),
+                        ("av", NS), ("bv", NS), ("mn", NS), ("mxv", NS), ("spr", NS), ("sp5", NS), ("ab", NS), ("c1", NS), ("c2", NS), ("tg", NS),
+                        ("dc", MS), ("dup", MS), ("dp1", MS), ("ntf", MS), ("lk2", MS), ("offf", MS), ("sx2", NS)])
+_pack("ki", "int32", [("ia", C), ("ib", C), ("ic", 512), ("ic2", 512), ("id1", 32), ("id2", 32), ("ie", 8), ("ig", 8), ("if1", NS), ("if2", 8), ("ih", 32)])
+for _n, _w in (("offrep", NS), ("offu", 8), ("offq", NS), ("offt", NS), ("offs", NS), ("offr", NS), ("offc", MS), ("offl", NS), ("offd", MS), ("offx", NS)):
+    _sb(_n, _w, "uint16")
+for _n in ("pss", "psa", "psm", "psr", "pd0", "pd1", "pd2", "pd3"):
+    SCRATCH[_n] = ("psum", [128, 512], "float32")
+
+SEMAPHORES = ["sv", "ss", "sg", "st"] + ["arr%d" % t for t in range(R)] + ["snd%d" % t for t in range(R)] + ["d%d" % i for i in range(18)]
+
+
+def make_queues(g, T):
+    eng = {"v": g.vector, "s": g.scalar, "g": g, "t": g.tensor, "y": g.sync}
+    sem = {"v": "sv", "s": "ss", "g": "sg", "t": "st"}
+    count = {k: 0 for k in sem}
+    known = {k: {} for k in eng}
+    snap = {}
+    log = {}
+    ndma = [0]
+
+    def psum(v):
+        return SCRATCH[v[0]][0] == "psum"
+
+    def region(v):
+        return (0, 512, 1) if psum(v) else (v[1], v[2], v[3])
+
+    def hit(p, q):
+        if p[0] >= q[1] or q[0] >= p[1]:
+            return False
+        return not (p[2] == q[2] and p[2] > 1 and (p[0] - q[0]) % p[2])
+
+    def wait(e, src, n):
+        if known[e].get(src, 0) >= n:
+            return
+        eng[e].wait_ge(T.sem[sem.get(src, src)], n)
+        known[e][src] = n
+        for k, m in snap.get((src, n), {}).items():
+            if known[e].get(k, 0) < m:
+                known[e][k] = m
+
+    def deps(e, outs, ins):
+        need = {}
+        for write, vs in ((True, outs), (False, ins)):
+            for v in vs:
+                r = region(v)
+                for w2, r2, src, n in log.get(v[0], []):
+                    if not hit(r, r2) or (e == "t" and src == "t"):
+                        continue
+                    if write or w2 or (psum(v) and src != e):
+                        need[src] = max(need.get(src, 0), n)
+        for src in sorted(need):
+            wait(e, src, need[src])
+
+    def record(outs, ins, src, n):
+        for write, vs in ((True, outs), (False, ins)):
+            for v in vs:
+                r = region(v)
+                L = log.setdefault(v[0], [])
+                if write and not psum(v) and r[2] == 1:
+                    L[:] = [x for x in L if not (r[0] <= x[1][0] and x[1][1] <= r[1])]
+                L[:] = [x for x in L if not (x[0] == write and x[1] == r and x[2] == src)]
+                L.append((write, r, src, n))
+
+    def ap(v):
+        x = T[v[0]][:, v[1]:v[2]:v[3]] if v[3] > 1 else T[v[0]][:, v[1]:v[2]]
+        if len(v) > 4:
+            if v[5] == "codes":
+                x = x.bitcast(dt.uint32)
+            if v[4] is not None:
+                o = v[4]
+                x = x.indirect(T[o[0]][:, o[1]:o[2]])
+        return x
+
+    def issue(e, outs, ins, call):
+        deps(e, outs, ins)
+        count[e] += 1
+        call().then_inc(T.sem[sem[e]], 1)
+        snap[(e, count[e])] = dict(known[e])
+        record(outs, ins, e, count[e])
+
+    def dma(e, out, in_, outs, ins, **kw):
+        deps(e, outs, ins)
+        name = "d%d" % ndma[0]
+        ndma[0] += 1
+        snap[(name, 16)] = dict(known[e])
+        eng[e].dma_start(out, in_, **kw).then_inc(T.sem[name], 16)
+        record(outs, ins, name, 16)
+
+    def finish():
+        for i in range(ndma[0]):
+            wait("g", "d%d" % i, 16)
+        for k in ("v", "s", "t", "g"):
+            wait("g", k, count[k])
+
+    return issue, dma, ap, wait, deps, finish
+
+
+def rank_program(g, core, T, topo):
+    rank = T.rank_of(core)
+    if rank is None:
+        return
+    issue, dma, ap, wait, deps, finish = make_queues(g, T)
+
+    def B(name, a=0, b=None, s=1):
+        if name in ALIAS:
+            buf, at, w = ALIAS[name]
+        else:
+            buf, at, w = name, 0, SCRATCH[name][1][1]
+        return (buf, at + a, at + (w if b is None else b), s)
+
+    def I(v, off, kind=""):
+        return v + (off, kind)
+
+    def srcs(*vs):
+        r = []
+        for v in vs:
+            r.append(v)
+            if len(v) > 4 and v[4] is not None:
+                r.append(v[4])
+        return r
+
+    def tt(out, a, b, op):
+        issue("v", [out], srcs(a, b), lambda: g.vector.tensor_tensor(ap(out), ap(a), ap(b), op))
+
+    def sc(out, a, s1, op0, s2=None, op1=None):
+        ins = srcs(a) + ([s1] if isinstance(s1, tuple) else [])
+        x1 = ap(s1) if isinstance(s1, tuple) else s1
+        if op1 is None:
+            issue("v", [out], ins, lambda: g.vector.tensor_scalar(ap(out), ap(a), x1, None, op0))
+        else:
+            issue("v", [out], ins, lambda: g.vector.tensor_scalar(ap(out), ap(a), x1, s2, op0, op1))
+
+    def scan(out, d0, d1, op0, op1):
+        issue("v", [out], [d0, d1], lambda: g.vector.tensor_tensor_scan(ap(out), ap(d0), ap(d1), 0.0, op0, op1))
+
+    def vcopy(out, a):
+        ins = srcs(a) + ([out[4]] if len(out) > 4 and out[4] is not None else [])
+        issue("v", [out], ins, lambda: g.vector.tensor_copy(ap(out), ap(a)))
+
+    def act(out, a, func=AF.Copy, scale=None, bias=None, acc=None):
+        kw = {}
+        ins, outs = srcs(a), [out]
+        for k, v in (("scale", scale), ("bias", bias)):
+            if v is not None:
+                kw[k] = ap(v) if isinstance(v, tuple) else v
+                if isinstance(v, tuple):
+                    ins.append(v)
+        if acc is not None:
+            kw["accum_out"] = ap(acc)
+            outs.append(acc)
+        issue("s", outs, ins, lambda: g.scalar.activation(ap(out), ap(a), func, **kw))
+
+    nj = [0]
+
+    def count_ones(acc, v, n):
+        nj[0] = (nj[0] + 1) % 3
+        act(B("junk%d" % nj[0], 0, n), v, acc=acc)
+
+    def fill(v, c):
+        issue("v", [v], [], lambda: g.vector.memset(ap(v), c))
+
+    def quant(name, n, tile):
+        src, o, s = B(tile, 0, 4 * n), B("q" + name, 0, n), B("s" + name, 0, n)
+        issue("v", [o, s], [src], lambda: g.vector.quantize_mx(ap(o), ap(s), ap(src)))
+
+    def mm(out, n, l, r, start=True, stop=True, la=0):
+        o = B(out, 0, n)
+        a, asc, b, bsc = B("q" + l, la, la + 128), B("s" + l, la, la + 128), B("q" + r, 0, n), B("s" + r, 0, n)
+        issue("t", [o], [a, asc, b, bsc], lambda: g.tensor.matmul_mx(ap(o), ap(a), ap(asc), ap(b), ap(bsc), start, stop))
+
+    def iota(v, pattern, base, cm):
+        kw = {} if SCRATCH[v[0]][2] == "int32" else {"allow_small_or_imprecise_dtypes": True}
+        issue("g", [v], [], lambda: g.iota(ap(v), pattern, base, cm, **kw))
+
+    def sel(out, in_, pattern, op, base, cm):
+        issue("g", [out], [in_], lambda: g.affine_select(ap(out), ap(in_), pattern, op, 0.0, base, cm))
+
+    def last16(name, n=C):
+        return B(name, 15, n, 16)
+
+    def mask(out, v, n=C):
+        scan(B(out, 0, n), v, B("mk", 0, n), OP.add, OP.mult)
+
+    def hold(out, m, n=C):
+        scan(B(out, 0, n), B("rst", 0, n), B(m, 0, n), OP.mult, OP.add)
+
+    dma("y", T["xa"][:, :], T.x[:, :], [B("xa")], [])
+    dma("s", T["ut"][:, :], T.u[:, :], [B("ut")], [])
+    dma("y", T["qw"][:, 0:512].bitcast(dt.uint8), T.wc[:, :], [B("qw")], [])
+    dma("s", T["sw"][:, :], T.ws[:, :], [B("sw")], [])
+    dma("y", T["vt"][:, :], T.v[:, :], [B("vt")], [])
+
+    iota(B("if2"), [[16, 8]], 0, 0)
+    iota(B("ia"), [[0, NS], [-1, 16]], 1024, 1)
+    iota(B("i16"), [[0, NS], [1, 16]], 0, 0)
+    iota(B("if1"), [[16, NS]], 15, 0)
+    fill(B("ctile"), 1.0)
+    vcopy(B("offu"), B("if2"))
+    fill(B("ct6"), 0.0)
+    sc(B("ib"), B("ia"), 15, OP.bitwise_and)
+    sc(B("mk"), B("ib"), 0.0, OP.is_equal)
+    sc(B("rst"), B("i16"), 1.0, OP.min)
+    vcopy(B("offrep"), B("if1"))
+    quant("u", 128, "ut")
+    vcopy(I(B("qux"), None, "codes"), I(B("qu"), B("offu"), "codes"))
+    act(B("sux"), I(B("su"), B("offu")))
+    quant("x", C, "xa")
+
+    sel(B("fb"), B("ctile"), [[-16, 8], [0, 16], [0, 4]], OP.is_ge, 0, 1)
+    sel(B("sgt"), B("fb"), [[16, 8], [0, 16], [0, 4]], OP.is_ge, 15, -1)
+    sel(B("fst"), B("ctile"), [[16, 8], [1, 16], [-1000, 4]], OP.is_gt, 0, -1)
+    sel(B("fst"), B("fst"), [[-16, 8], [0, 16], [0, 4]], OP.is_ge, 0, 1)
+    sel(B("fb"), B("ctile"), [[-16, 8], [-1, 16], [1000, 4]], OP.is_gt, -1000, 1)
+    sel(B("fb"), B("fb"), [[0, 8], [0, 16], [-1, 4]], OP.is_ge, 1, 0)
+    sel(B("fb"), B("fb"), [[16, 8], [0, 16], [0, 4]], OP.is_ge, 15, -1)
+    for q in (3, 2, 1, 0):
+        iota(B("ct%d" % q), [[0, 4 * QN[q]]], 0, 0)
+    iota(B("cst"), [[-16, NS]], 208, 0)
+    iota(B("iotaj"), [[1, C]], -224, 0)
+    iota(B("ie"), [[-16, 8]], 0, 1)
+    iota(B("ic"), [[-1, 128], [0, 4]], 1024, 1)
+    iota(B("id1"), [[0, 4], [-16, 8]], 0, 1)
+    iota(B("ih"), [[0, 4], [1, 8]], 0, 0)
+    for b in range(4):
+        sel(B("et%d" % b), B("ctile"), [[-4, 128], [-1, 4]], OP.is_equal, b, 4)
+    iota(B("iot512"), [[512, C]], 0, 0)
+    iota(B("kca"), [[-1, C]], C - 1, 0)
+    iota(B("kv"), [[1, M]], 0, 0)
+
+    def consts_first():
+        sc(B("sgt"), B("sgt"), -1.0, OP.mult)
+        quant("sg", 128, "sgt")
+        fill(B("ft"), 0.0)
+        fill(B("ct5"), 0.0)
+        fill(B("ct4"), 0.0)
+        fill(B("rs", 0, 1), 0.0)
+
+    def consts_mid():
+        tt(B("fst"), B("fst"), B("fb"), OP.add)
+        quant("fs", 128, "fst")
+
+    def consts_last():
+        fill(B("dg"), 0.0)
+        sc(B("ig"), B("ie"), 4, OP.arith_shift_right)
+        sc(B("gm"), B("ig"), 0.0, OP.is_equal)
+        sc(B("ic2"), B("ic"), 15, OP.bitwise_and)
+        sc(B("mst"), B("ic2"), 0.0, OP.is_equal)
+        quant("ms", 128, "mst")
+        mask("jwm", B("iotaj"))
+        hold("jwf", "jwm")
+        sc(B("j448"), last16("jwf"), -224.0, OP.add)
+        sc(B("kc"), last16("jwf"), -1.0, OP.mult, 223.0, OP.add)
+        sc(B("nt"), last16("jwf", M), 672.0, OP.add)
+        sc(B("id2"), B("id1"), 4, OP.arith_shift_right)
+        sc(B("mb"), B("id2"), 0.0, OP.is_equal)
+        sc(B("rst8"), B("ih"), 1.0, OP.min)
+        fill(B("ont"), 0.5)
+        o = B("ont", 3, 512, 4)
+        issue("v", [o], [], lambda: g.vector.memset(T[o[0]][0:64, o[1]:o[2]:o[3]], 0.0))
+        quant("on", 128, "ont")
+        hold("jwm", "mk", M)
+        sc(B("bigm"), B("jwm", 0, M), 1000.0, OP.mult)
+        fill(B("dc", 0, 1), 0.0)
+        quant("v", 128, "vt")
+        for b in range(4):
+            quant("e%d" % b, 128, "et%d" % b)
+
+    X = ["xa", "xb"]
+    for t in range(R):
+        x, xn = X[t % 2], X[(t + 1) % 2]
+        first = t == 0
+        mm("pss", C, "ux", "x")
+        if not first:
+            for b in range(4):
+                mm("pd%d" % b, C, "e%d" % b, "x")
+        tt(B("sm"), B("pss", 0, C), B("mk"), OP.mult)
+        hold("swf", "sm")
+        if not first:
+            act(B("t0"), B("pd0", 0, C))
+        act(B("rep"), I(B("swf"), B("offrep")))
+        for q in (6, 5, 4, 3, 2, 1, 0):
+            for k in range(4 * q + 3, max(4 * q - 1, 0), -1):
+                c = B("ct%d" % q, k % 4, 64 * k, 4)
+                sc(c, B("pss", 0, 16 * k), B("swf", 16 * k + 15, 16 * k + 16), OP.is_ge)
+                count_ones(B("rs", k, k + 1), c, 16 * k)
+            if first and q == 6:
+                consts_first()
+            quant("c%d" % q, QN[q], "ct%d" % q)
+            mm("psa", QN[q], "sg", "c%d" % q, q == 6, q == 0)
+            if q == 4:
+                if first:
+                    consts_mid()
+                tt(B("ft", 0, 4 * C, 4), B("pss", 0, C), B("rep"), OP.is_le)
+                tt(B("ft", 1, 4 * C, 4), B("pss", 0, C), B("rep"), OP.is_lt)
+                quant("f", C, "ft")
+                mm("psa", C, "fs", "f", False, False)
+            if q == 1 and first:
+                consts_last()
+        if first:
+            for b in range(4):
+                mm("pd%d" % b, C, "e%d" % b, "x")
+            act(B("t0"), B("pd0", 0, C))
+        act(B("t1"), B("pd1", 0, C))
+        tt(B("em"), B("psa", 0, C), B("mk"), OP.mult)
+        hold("ef", "em")
+        tt(B("rsc"), B("rs"), B("cst"), OP.add)
+        tt(B("z"), last16("ef"), B("rsc"), OP.add)
+        sc(B("x1"), B("z"), 0.0625, OP.mult, MAGIC, OP.add)
+        sc(B("dg", 0, 112, 4), B("x1"), -MAGIC, OP.add, 16.0, OP.mult)
+        tt(B("dg", 1, 112, 4), B("z"), B("dg", 0, 112, 4), OP.subtract)
+        for gr in range(4):
+            act(B("mv", 112 * (gr + 4), 112 * (gr + 5)), B("dg"), scale=B("gm", gr + 4, gr + 5))
+            sc(B("mv", 112 * gr, 112 * (gr + 1)), B("dg"), B("gm", gr, gr + 1), OP.mult)
+        quant("mv", 224, "mv")
+        mm("psm", 224, "ms", "mv")
+        act(B("t2"), B("pd2", 0, C))
+        act(B("t3"), B("pd3", 0, C))
+        sc(B("offq"), B("z"), 224.0, OP.add)
+        vcopy(I(B("ot"), B("offq")), B("iotaj"))
+        vcopy(B("m8"), B("psm", 112, 224))
+        tt(B("lo"), B("psm", 0, 112), B("m8"), OP.min)
+        tt(B("hi"), B("psm", 0, 112), B("m8"), OP.max)
+        tt(B("gg", 0, 56), B("lo", 0, 56), B("lo", 56, 112), OP.min)
+        tt(B("gg", 168, 224), B("hi", 0, 56), B("hi", 56, 112), OP.max)
+        tt(B("mn"), B("gg", 0, 28), B("gg", 28, 56), OP.min)
+        tt(B("mxv"), B("gg", 168, 196), B("gg", 196, 224), OP.max)
+        tt(B("gx"), B("lo", 0, 56), B("lo", 56, 112), OP.max)
+        tt(B("spr"), B("mxv"), B("mn"), OP.subtract)
+        tt(B("gy"), B("hi", 0, 56), B("hi", 56, 112), OP.min)
+        sc(B("offs"), B("spr"), 0.0, OP.add)
+        sc(B("sp5"), B("spr"), 512.0, OP.mult)
+        tt(B("ka"), I(B("iot512"), B("offs")), B("kca"), OP.add)
+        tt(B("kw"), B("sp5"), B("kc"), OP.add)
+        tt(B("km", 0, 24), B("kw", 0, 24), B("mb", 0, 24), OP.mult)
+        tt(B("km", 24, 32), B("kw", 20, 28), B("mb", 24, 32), OP.mult)
+        scan(B("kf"), B("rst8"), B("km"), OP.mult, OP.add)
+        for e in range(4):
+            act(B("cr", e, 4 * C, 4), B("ka"), AF.Sign, scale=-1.0, bias=B("kf", 8 * e + 7, 8 * e + 8))
+        tt(B("gg", 56, 112), B("gx"), B("gy"), OP.min)
+        tt(B("gg", 112, 168), B("gx"), B("gy"), OP.max)
+        for r in range(4):
+            p, o = B("gg", 56 * r, 56 * r + 28), B("gg", 56 * (3 - r) + 28, 56 * (3 - r) + 56)
+            tt(B("aa", 28 * r, 28 * r + 28), p, o, OP.min)
+            tt(B("bb", 28 * r, 28 * r + 28), p, o, OP.max)
+        tt(B("a2"), B("aa", 0, 56), B("aa", 56, 112), OP.max)
+        tt(B("b2"), B("bb", 0, 56), B("bb", 56, 112), OP.min)
+        tt(B("av"), B("a2", 0, 28), B("a2", 28, 56), OP.max)
+        tt(B("bv"), B("b2", 0, 28), B("b2", 28, 56), OP.min)
+        tt(B("c1"), B("z"), B("av"), OP.max)
+        tt(B("ab"), B("av"), B("bv"), OP.add)
+        tt(B("c2"), B("c1"), B("bv"), OP.min)
+        tt(B("tg"), B("ab"), B("c2"), OP.subtract)
+        sc(B("offt"), B("tg"), 224.0, OP.add)
+        quant("cr", C, "cr")
+        mm("psr", C, "on", "cr")
+        vcopy(B("la"), I(B("ot"), B("offt")))
+        mask("lm", B("la"))
+        hold("lf", "lm")
+        sc(B("offl"), last16("lf"), 224.0, OP.add)
+        for b in range(4):
+            act(B("tl", b, 4 * C, 4), I(B("t%d" % b), B("offl")))
+        tt(B("em2"), B("psr", 0, C), B("mk"), OP.mult)
+        hold("rf", "em2")
+        sc(B("offr"), last16("rf"), 223.5, OP.add)
+        vcopy(I(B("ctab"), B("offr")), B("iotaj"))
+        mask("cm", B("ctab", 0, M), M)
+        hold("cf", "cm", M)
+        sc(B("offc"), last16("cf", M), 224.0, OP.add)
+        n_tl, n_z, n_a = "tl%d" % t, "z%d" % t, "a%d" % t
+        vcopy(B("lk"), I(B("la"), B("offc")))
+        quant(n_tl, C, "tl")
+        act(B("s" + n_z), I(B("s" + n_tl), B("offc")))
+        vcopy(I(B("q" + n_z), None, "codes"), I(B("q" + n_tl), B("offc"), "codes"))
+        to = T.cores[(rank + 1 + t) % len(T.cores)]
+        rid, pid, _se = topo.addr(to)
+        en = topo.engines(core, to)
+        wide, thin = en[0::2], en[1::4]
+        got = len(wide) + len(thin)
+        for nm, view, es in (("s", lambda n: T["s" + n][:, 0:M], thin), ("q", lambda n: T["q" + n][:, 0:M].bitcast(dt.uint8), wide)):
+            deps("g", [], [B(nm + n_z)])
+            g.remote_dma(view(n_a), view(n_z), T.sem["arr%d" % t], T.sem["snd%d" % t], pid, rid, sum(1 << e for e in es))
+        dma("g", T[x][:, :], T["tl"][:, :], [B(x)], [B("tl")], accum_op=OP.add)
+        iota(B("st", 0, C), [[0, C]], -512, 0)
+        mask("lkm", B("lk"), M)
+        hold("lkf", "lkm", M)
+        for k in range(MS - 1, 0, -1):
+            e = B("eqo", 192 * k, 192 * k + 16 * k)
+            sc(e, B("lk", 0, 16 * k), B("lkf", 16 * k + 15, 16 * k + 16), OP.is_equal)
+            count_ones(B("dc", k, k + 1), e, 16 * k)
+        if t == R - 1:
+            act(B("olf"), B("la"), AF.Identity, bias=224.0)
+            dma("y", T.ol[:, :], T["olf"][0:128:16, :], [], [B("olf")])
+        tt(B("rep2"), I(B("lkf"), B("offrep", 0, MS)), B("bigm"), OP.add)
+        tt(B("eqd"), B("lk"), B("rep2"), OP.is_equal)
+        scan(B("df"), B("rst", 0, M), B("eqd"), OP.mult, OP.max)
+        sc(B("lk2"), last16("lkf", M), 224.0, OP.add)
+        tt(B("dup"), B("dc"), last16("df", M), OP.max)
+        sc(B("dp1"), B("dup"), 1.0, OP.min)
+        tt(B("ntf"), B("dp1"), B("nt"), OP.mult)
+        tt(B("offf"), B("ntf"), B("lk2"), OP.max)
+        sc(B("offd"), B("offf"), 0.0, OP.add)
+        vcopy(I(B("st"), B("offd")), B("kv"))
+        mask("stm", B("st", 0, C))
+        hold("stf", "stm")
+        tt(B("sx2"), last16("stf"), B("j448"), OP.max)
+        sc(B("offx"), B("sx2"), 448.0, OP.add)
+        for b in range(4):
+            o, i = B("yh%d" % b, 0, C), B(x, b, 4 * C, 4)
+            if b % 2:
+                act(o, i, scale=0.5)
+            else:
+                sc(o, i, 0.5, OP.mult)
+        wait("t", "arr%d" % t, got)
+        for b in range(4):
+            mm("pd%d" % b, M, "w", n_a, la=128 * b)
+        for b in range(4):
+            h, pd = B("yh%d" % b, C, C + M), B("pd%d" % b, 0, M)
+            if b % 2:
+                act(h, pd, scale=0.03125)
+            else:
+                sc(h, pd, 0.03125, OP.mult)
+        for b in range(4):
+            o, w = B(xn, b, 4 * C, 4), I(B("yh%d" % b), B("offx"))
+            if b % 2:
+                act(o, w)
+            else:
+                vcopy(o, w)
+        quant("x", C, xn)
+    mm("pss", C, "v", "x")
+    act(B("yo"), B("pss", 0, C))
+    dma("y", T.oc[:, :], T["qx"][:, 0:C].bitcast(dt.uint8), [], [B("qx")])
+    for k in range(4):
+        dma("y", T.osc[4 * k:4 * k + 4, :], T["sx"][32 * k:32 * k + 4, 0:C], [], [B("sx")])
+    dma("s", T.y[:, :], T["yo"][:, :], [], [B("yo")])
+    for t in range(R):
+        wait("g", "arr%d" % t, got)
+        wait("g", "snd%d" % t, got)
+    finish()

@@ -3,6 +3,7 @@ from concourse.mybir import dt, AluOpType, ActivationFunctionType
 C, M, R, NS, MS = 448, 192, 3, 28, 12
 MAGIC = 12582912.0
 QN = [128, 128, 176, 240, 304, 368, 448]
+BYSIGN = (24, 20, 19, 16, 12)
 OP = AluOpType
 AF = ActivationFunctionType
 
@@ -40,11 +41,12 @@ for _n in ("xa", "xb", "ft", "cr", "tl"):
     _sb(_n, 4 * C, "bfloat16")
 _sb("ut", 512, "bfloat16")
 _sb("vt", 512, "bfloat16")
-_pack("kt", "bfloat16", [(n, 512) for n in ("ctile", "fb", "sgt", "fst", "mst", "ont", "et0", "et1", "et2", "et3")])
+_pack("kt", "bfloat16", [(n, 512) for n in ("ctile", "cneg", "fb", "sgt", "fst", "mst", "ont", "et0", "et1", "et2", "et3")])
 _pack("tb", "bfloat16", [("t%d" % b, C) for b in range(4)])
 _pack("yh", "bfloat16", [("yh%d" % b, C + M) for b in range(4)])
 _pack("ctb", "bfloat16", [("ct%d" % q, 4 * QN[q]) for q in range(7)])
-_pack("kb", "bfloat16", [("mk", C), ("rst", C), ("iotaj", C), ("bigm", M), ("kv", M), ("i16", C), ("jwm", C), ("jwf", C)])
+_pack("kb", "bfloat16", [("mk", C), ("rst", C), ("iotaj", C), ("mlt", M), ("kv", M), ("i16", C), ("jwm", C), ("jwf", C)])
+_pack("sgn", "bfloat16", [("sgn%d" % k, 16 * k) for k in BYSIGN])
 _packmx("k", [(n, 128) for n in ("e0", "e1", "e2", "e3", "sg", "fs", "ms", "on")])
 _packmx("c", [("c%d" % q, QN[q]) for q in range(7)])
 for _n, _w in (("u", 128), ("ux", 128), ("v", 128), ("w", 512), ("x", C), ("f", C), ("mv", 224), ("cr", C)):
@@ -54,22 +56,22 @@ for _t in range(R):
     _mx("z%d" % _t, M)
     _mx("a%d" % _t, M)
 for _n, _w in (("junk0", C), ("junk1", C), ("junk2", C), ("ot", C), ("la", C), ("lm", C), ("lf", C), ("ctab", C), ("cm", M), ("cf", M), ("lk", M), ("lkm", M),
-               ("lkf", M), ("rep2", M), ("eqd", M), ("df", M), ("eqo", 12 * 192), ("st", C + M), ("stm", C), ("stf", C), ("dg", 112),
-               ("mv", 896), ("m8", 112), ("lo", 112), ("hi", 112), ("gx", 56), ("gy", 56), ("gg", 224)):
+               ("lkf", M), ("rep2", M), ("eqd", M), ("eqm", M), ("df", M), ("eqo", 12 * 192), ("st", C + M), ("stm", C), ("stf", C), ("rfb", C), ("em2", C),
+               ("rf", C), ("dg", 112), ("mv", 896), ("m8", 112), ("lo", 112), ("hi", 112), ("gx", 56), ("gy", 56), ("gg", 224)):
     _sb(_n, _w, "bfloat16")
-for _n in ("sm", "swf", "rep", "em", "ef", "em2", "rf", "iot512", "kca", "ka", "yo", "olf"):
+for _n in ("sm", "swf", "rep", "em", "ef", "iot512", "kca", "ka", "yo", "olf"):
     _sb(_n, C, "float32")
-_pack("fk", "float32", [("cst", NS), ("gm", 8), ("mb", 32), ("rst8", 32), ("kc", NS), ("j448", NS), ("nt", MS)])
+_pack("fk", "float32", [("cst", NS), ("onef", 32), ("gm", 8), ("mb", 32), ("rst8", 32), ("kc", NS), ("j448", NS), ("nt", MS)])
 _pack("fw", "float32", [("rs", NS), ("rsc", NS), ("z", NS), ("x1", NS), ("kw", NS), ("km", 32), ("kf", 32), ("aa", 112), ("bb", 112), ("a2", 56), ("b2", 56),
                         ("av", NS), ("bv", NS), ("mn", NS), ("mxv", NS), ("spr", NS), ("sp5", NS), ("ab", NS), ("c1", NS), ("c2", NS), ("tg", NS),
                         ("dc", MS), ("dup", MS), ("dp1", MS), ("ntf", MS), ("lk2", MS), ("offf", MS), ("sx2", NS)])
-_pack("ki", "int32", [("ia", C), ("ib", C), ("ic", 512), ("ic2", 512), ("id1", 32), ("id2", 32), ("ie", 8), ("ig", 8), ("if1", NS), ("if2", 8), ("ih", 32)])
+_pack("ki", "int32", [("ia", C), ("ib", C), ("if1", NS), ("if2", 8)])
 for _n, _w in (("offrep", NS), ("offu", 8), ("offq", NS), ("offt", NS), ("offs", NS), ("offr", NS), ("offc", MS), ("offl", NS), ("offd", MS), ("offx", NS)):
     _sb(_n, _w, "uint16")
 for _n in ("pss", "psa", "psm", "psr", "pd0", "pd1", "pd2", "pd3"):
     SCRATCH[_n] = ("psum", [128, 512], "float32")
 
-SEMAPHORES = ["sv", "ss", "sg", "st"] + ["arr%d" % t for t in range(R)] + ["snd%d" % t for t in range(R)] + ["d%d" % i for i in range(18)]
+SEMAPHORES = ["sv", "ss", "sg", "st"] + ["arr%d" % t for t in range(R)] + ["snd%d" % t for t in range(R)] + ["d%d" % i for i in range(24)]
 
 
 def make_queues(g, T):
@@ -253,13 +255,25 @@ def rank_program(g, core, T, topo):
     dma("s", T["sw"][:, :], T.ws[:, :], [B("sw")], [])
     dma("y", T["vt"][:, :], T.v[:, :], [B("vt")], [])
 
+    def zeros(n):
+        w = ALIAS[n][2]
+        for a in range(0, w, 512):
+            act(B(n, a, min(a + 512, w)), B("ctile", 0, min(512, w - a)), scale=0.0)
+
     iota(B("if2"), [[16, 8]], 0, 0)
     iota(B("ia"), [[0, NS], [-1, 16]], 1024, 1)
     iota(B("i16"), [[0, NS], [1, 16]], 0, 0)
     iota(B("if1"), [[16, NS]], 15, 0)
     fill(B("ctile"), 1.0)
+    zeros("ct6")
+    fill(B("ft"), 0.0)
+    for a, b in (("ct4", "ct4"), ("ct3", "ct3"), ("ct0", "ct2")):
+        n = ALIAS[b][1] + ALIAS[b][2] - ALIAS[a][1]
+        o, i = B(a, 0, n), B("ft", 0, n)
+        dma("y", ap(o), ap(i), [o], [i])
+    fill(B("cneg"), -1.0)
     vcopy(B("offu"), B("if2"))
-    fill(B("ct6"), 0.0)
+    fill(B("fst"), 0.0)
     sc(B("ib"), B("ia"), 15, OP.bitwise_and)
     sc(B("mk"), B("ib"), 0.0, OP.is_equal)
     sc(B("rst"), B("i16"), 1.0, OP.min)
@@ -268,71 +282,55 @@ def rank_program(g, core, T, topo):
     vcopy(I(B("qux"), None, "codes"), I(B("qu"), B("offu"), "codes"))
     act(B("sux"), I(B("su"), B("offu")))
     quant("x", C, "xa")
+    zeros("ct5")
 
-    sel(B("fb"), B("ctile"), [[-16, 8], [0, 16], [0, 4]], OP.is_ge, 0, 1)
+    sel(B("fb"), B("cneg"), [[-16, 8], [0, 16], [0, 4]], OP.is_ge, 0, 1)
     sel(B("sgt"), B("fb"), [[16, 8], [0, 16], [0, 4]], OP.is_ge, 15, -1)
-    sel(B("fst"), B("ctile"), [[16, 8], [1, 16], [-1000, 4]], OP.is_gt, 0, -1)
-    sel(B("fst"), B("fst"), [[-16, 8], [0, 16], [0, 4]], OP.is_ge, 0, 1)
-    sel(B("fb"), B("ctile"), [[-16, 8], [-1, 16], [1000, 4]], OP.is_gt, -1000, 1)
-    sel(B("fb"), B("fb"), [[0, 8], [0, 16], [-1, 4]], OP.is_ge, 1, 0)
-    sel(B("fb"), B("fb"), [[16, 8], [0, 16], [0, 4]], OP.is_ge, 15, -1)
-    for q in (3, 2, 1, 0):
-        iota(B("ct%d" % q), [[0, 4 * QN[q]]], 0, 0)
+    l0, l1, one = B("fst", 0, 512, 4), B("fst", 1, 512, 4), B("ctile", 0, 128)
+    sel(l0, one, [[16, 8], [1, 16]], OP.is_gt, 0, -1)
+    sel(l0, l0, [[-16, 8], [0, 16]], OP.is_ge, 0, 1)
+    sel(l1, one, [[-16, 8], [-1, 16]], OP.is_gt, 0, 1)
+    sel(l1, l1, [[16, 8], [0, 16]], OP.is_ge, 15, -1)
+    iota(B("rs", 0, 1), [[0, 1]], 0, 0)
+    iota(B("dc", 0, 1), [[0, 1]], 0, 0)
     iota(B("cst"), [[-16, NS]], 208, 0)
     iota(B("iotaj"), [[1, C]], -224, 0)
-    iota(B("ie"), [[-16, 8]], 0, 1)
-    iota(B("ic"), [[-1, 128], [0, 4]], 1024, 1)
-    iota(B("id1"), [[0, 4], [-16, 8]], 0, 1)
-    iota(B("ih"), [[0, 4], [1, 8]], 0, 0)
+    iota(B("dg"), [[0, 112]], 0, 0)
+    iota(B("onef"), [[0, 32]], 1, 0)
+    sel(B("gm"), B("onef", 0, 8), [[-16, 8]], OP.is_ge, 0, 1)
+    sel(B("gm"), B("gm"), [[16, 8]], OP.is_ge, 15, -1)
+    sel(B("mb"), B("onef"), [[0, 4], [-16, 8]], OP.is_ge, 0, 1)
+    sel(B("mb"), B("mb"), [[0, 4], [16, 8]], OP.is_ge, 15, -1)
+    sel(B("rst8"), B("onef"), [[0, 4], [1, 8]], OP.is_gt, 0, 0)
     for b in range(4):
         sel(B("et%d" % b), B("ctile"), [[-4, 128], [-1, 4]], OP.is_equal, b, 4)
+    sel(B("ont"), B("ctile"), [[0, 128], [-1000, 4]], OP.is_ge, 2936, 1)
     iota(B("iot512"), [[512, C]], 0, 0)
     iota(B("kca"), [[-1, C]], C - 1, 0)
     iota(B("kv"), [[1, M]], 0, 0)
 
-    def consts_first():
-        sc(B("sgt"), B("sgt"), -1.0, OP.mult)
-        quant("sg", 128, "sgt")
-        fill(B("ft"), 0.0)
-        fill(B("ct5"), 0.0)
-        fill(B("ct4"), 0.0)
-        fill(B("rs", 0, 1), 0.0)
-
-    def consts_mid():
-        tt(B("fst"), B("fst"), B("fb"), OP.add)
-        quant("fs", 128, "fst")
-
     def consts_last():
-        fill(B("dg"), 0.0)
-        sc(B("ig"), B("ie"), 4, OP.arith_shift_right)
-        sc(B("gm"), B("ig"), 0.0, OP.is_equal)
-        sc(B("ic2"), B("ic"), 15, OP.bitwise_and)
-        sc(B("mst"), B("ic2"), 0.0, OP.is_equal)
-        quant("ms", 128, "mst")
+        for e in range(4):
+            act(B("mst", e, 512, 4), B("mk", 0, 128))
         mask("jwm", B("iotaj"))
         hold("jwf", "jwm")
         sc(B("j448"), last16("jwf"), -224.0, OP.add)
         sc(B("kc"), last16("jwf"), -1.0, OP.mult, 223.0, OP.add)
         sc(B("nt"), last16("jwf", M), 672.0, OP.add)
-        sc(B("id2"), B("id1"), 4, OP.arith_shift_right)
-        sc(B("mb"), B("id2"), 0.0, OP.is_equal)
-        sc(B("rst8"), B("ih"), 1.0, OP.min)
-        fill(B("ont"), 0.5)
-        o = B("ont", 3, 512, 4)
-        issue("v", [o], [], lambda: g.vector.memset(T[o[0]][0:64, o[1]:o[2]:o[3]], 0.0))
-        quant("on", 128, "ont")
-        hold("jwm", "mk", M)
-        sc(B("bigm"), B("jwm", 0, M), 1000.0, OP.mult)
-        fill(B("dc", 0, 1), 0.0)
-        quant("v", 128, "vt")
+        quant("ms", 128, "mst")
         for b in range(4):
             quant("e%d" % b, 128, "et%d" % b)
+        quant("on", 128, "ont")
+        hold("jwm", "mk", M)
+        sc(B("mlt"), B("jwm", 0, M), -1.0, OP.mult, 1.0, OP.add)
+        quant("v", 128, "vt")
 
     X = ["xa", "xb"]
     for t in range(R):
         x, xn = X[t % 2], X[(t + 1) % 2]
         first = t == 0
         mm("pss", C, "ux", "x")
+        mm("psm", C, "ux", "x")
         if not first:
             for b in range(4):
                 mm("pd%d" % b, C, "e%d" % b, "x")
@@ -340,19 +338,32 @@ def rank_program(g, core, T, topo):
         hold("swf", "sm")
         if not first:
             act(B("t0"), B("pd0", 0, C))
-        act(B("rep"), I(B("swf"), B("offrep")))
+
+        def signs(q):
+            for k in range(4 * q + 3, 4 * q - 1, -1):
+                if k in BYSIGN:
+                    act(B("sgn%d" % k), B("psm", 0, 16 * k), AF.Sign, scale=-1.0, bias=B("swf", 16 * k + 15, 16 * k + 16))
+
+        signs(6)
         for q in (6, 5, 4, 3, 2, 1, 0):
             for k in range(4 * q + 3, max(4 * q - 1, 0), -1):
                 c = B("ct%d" % q, k % 4, 64 * k, 4)
-                sc(c, B("pss", 0, 16 * k), B("swf", 16 * k + 15, 16 * k + 16), OP.is_ge)
+                if k in BYSIGN:
+                    sc(c, B("sgn%d" % k), 0.0, OP.is_le)
+                else:
+                    sc(c, B("pss", 0, 16 * k), B("swf", 16 * k + 15, 16 * k + 16), OP.is_ge)
+                if k == 4 * q + 3:
+                    signs(q - 1)
                 count_ones(B("rs", k, k + 1), c, 16 * k)
+                if k == 23:
+                    act(B("rep"), I(B("swf"), B("offrep")))
             if first and q == 6:
-                consts_first()
+                quant("sg", 128, "sgt")
             quant("c%d" % q, QN[q], "ct%d" % q)
             mm("psa", QN[q], "sg", "c%d" % q, q == 6, q == 0)
             if q == 4:
                 if first:
-                    consts_mid()
+                    quant("fs", 128, "fst")
                 tt(B("ft", 0, 4 * C, 4), B("pss", 0, C), B("rep"), OP.is_le)
                 tt(B("ft", 1, 4 * C, 4), B("pss", 0, C), B("rep"), OP.is_lt)
                 quant("f", C, "ft")
@@ -365,10 +376,11 @@ def rank_program(g, core, T, topo):
             act(B("t0"), B("pd0", 0, C))
         act(B("t1"), B("pd1", 0, C))
         tt(B("em"), B("psa", 0, C), B("mk"), OP.mult)
-        hold("ef", "em")
         tt(B("rsc"), B("rs"), B("cst"), OP.add)
+        hold("ef", "em")
         tt(B("z"), last16("ef"), B("rsc"), OP.add)
         sc(B("x1"), B("z"), 0.0625, OP.mult, MAGIC, OP.add)
+        sc(B("offq"), B("z"), 224.0, OP.add)
         sc(B("dg", 0, 112, 4), B("x1"), -MAGIC, OP.add, 16.0, OP.mult)
         tt(B("dg", 1, 112, 4), B("z"), B("dg", 0, 112, 4), OP.subtract)
         for gr in range(4):
@@ -378,7 +390,6 @@ def rank_program(g, core, T, topo):
         mm("psm", 224, "ms", "mv")
         act(B("t2"), B("pd2", 0, C))
         act(B("t3"), B("pd3", 0, C))
-        sc(B("offq"), B("z"), 224.0, OP.add)
         vcopy(I(B("ot"), B("offq")), B("iotaj"))
         vcopy(B("m8"), B("psm", 112, 224))
         tt(B("lo"), B("psm", 0, 112), B("m8"), OP.min)
@@ -394,13 +405,13 @@ def rank_program(g, core, T, topo):
         sc(B("sp5"), B("spr"), 512.0, OP.mult)
         tt(B("ka"), I(B("iot512"), B("offs")), B("kca"), OP.add)
         tt(B("kw"), B("sp5"), B("kc"), OP.add)
+        tt(B("gg", 56, 112), B("gx"), B("gy"), OP.min)
         tt(B("km", 0, 24), B("kw", 0, 24), B("mb", 0, 24), OP.mult)
         tt(B("km", 24, 32), B("kw", 20, 28), B("mb", 24, 32), OP.mult)
+        tt(B("gg", 112, 168), B("gx"), B("gy"), OP.max)
         scan(B("kf"), B("rst8"), B("km"), OP.mult, OP.add)
         for e in range(4):
             act(B("cr", e, 4 * C, 4), B("ka"), AF.Sign, scale=-1.0, bias=B("kf", 8 * e + 7, 8 * e + 8))
-        tt(B("gg", 56, 112), B("gx"), B("gy"), OP.min)
-        tt(B("gg", 112, 168), B("gx"), B("gy"), OP.max)
         for r in range(4):
             p, o = B("gg", 56 * r, 56 * r + 28), B("gg", 56 * (3 - r) + 28, 56 * (3 - r) + 56)
             tt(B("aa", 28 * r, 28 * r + 28), p, o, OP.min)
@@ -416,21 +427,22 @@ def rank_program(g, core, T, topo):
         sc(B("offt"), B("tg"), 224.0, OP.add)
         quant("cr", C, "cr")
         mm("psr", C, "on", "cr")
+        act(B("rfb"), B("psr", 0, C), AF.Identity, scale=0.5, bias=-0.5)
         vcopy(B("la"), I(B("ot"), B("offt")))
         mask("lm", B("la"))
         hold("lf", "lm")
+        mask("em2", B("rfb"))
         sc(B("offl"), last16("lf"), 224.0, OP.add)
         for b in range(4):
             act(B("tl", b, 4 * C, 4), I(B("t%d" % b), B("offl")))
-        tt(B("em2"), B("psr", 0, C), B("mk"), OP.mult)
         hold("rf", "em2")
-        sc(B("offr"), last16("rf"), 223.5, OP.add)
+        sc(B("offr"), last16("rf"), 224.0, OP.add)
         vcopy(I(B("ctab"), B("offr")), B("iotaj"))
         mask("cm", B("ctab", 0, M), M)
         hold("cf", "cm", M)
         sc(B("offc"), last16("cf", M), 224.0, OP.add)
         n_tl, n_z, n_a = "tl%d" % t, "z%d" % t, "a%d" % t
-        vcopy(B("lk"), I(B("la"), B("offc")))
+        act(B("lk"), I(B("la"), B("offc")))
         quant(n_tl, C, "tl")
         act(B("s" + n_z), I(B("s" + n_tl), B("offc")))
         vcopy(I(B("q" + n_z), None, "codes"), I(B("q" + n_tl), B("offc"), "codes"))
@@ -446,6 +458,7 @@ def rank_program(g, core, T, topo):
         iota(B("st", 0, C), [[0, C]], -512, 0)
         mask("lkm", B("lk"), M)
         hold("lkf", "lkm", M)
+        act(B("rep2"), I(B("lkf"), B("offrep", 0, MS)))
         for k in range(MS - 1, 0, -1):
             e = B("eqo", 192 * k, 192 * k + 16 * k)
             sc(e, B("lk", 0, 16 * k), B("lkf", 16 * k + 15, 16 * k + 16), OP.is_equal)
@@ -453,26 +466,31 @@ def rank_program(g, core, T, topo):
         if t == R - 1:
             act(B("olf"), B("la"), AF.Identity, bias=224.0)
             dma("y", T.ol[:, :], T["olf"][0:128:16, :], [], [B("olf")])
-        tt(B("rep2"), I(B("lkf"), B("offrep", 0, MS)), B("bigm"), OP.add)
         tt(B("eqd"), B("lk"), B("rep2"), OP.is_equal)
-        scan(B("df"), B("rst", 0, M), B("eqd"), OP.mult, OP.max)
+        scan(B("eqm"), B("eqd"), B("mlt"), OP.max, OP.mult)
         sc(B("lk2"), last16("lkf", M), 224.0, OP.add)
+        scan(B("df"), B("rst", 0, M), B("eqm"), OP.mult, OP.max)
         tt(B("dup"), B("dc"), last16("df", M), OP.max)
         sc(B("dp1"), B("dup"), 1.0, OP.min)
         tt(B("ntf"), B("dp1"), B("nt"), OP.mult)
         tt(B("offf"), B("ntf"), B("lk2"), OP.max)
         sc(B("offd"), B("offf"), 0.0, OP.add)
         vcopy(I(B("st"), B("offd")), B("kv"))
-        mask("stm", B("st", 0, C))
-        hold("stf", "stm")
-        tt(B("sx2"), last16("stf"), B("j448"), OP.max)
-        sc(B("offx"), B("sx2"), 448.0, OP.add)
-        for b in range(4):
+
+        def halve(b):
             o, i = B("yh%d" % b, 0, C), B(x, b, 4 * C, 4)
             if b % 2:
                 act(o, i, scale=0.5)
             else:
                 sc(o, i, 0.5, OP.mult)
+
+        halve(1)
+        halve(3)
+        mask("stm", B("st", 0, C))
+        halve(0)
+        hold("stf", "stm")
+        halve(2)
+        tt(B("sx2"), last16("stf"), B("j448"), OP.max)
         wait("t", "arr%d" % t, got)
         for b in range(4):
             mm("pd%d" % b, M, "w", n_a, la=128 * b)
@@ -482,6 +500,8 @@ def rank_program(g, core, T, topo):
                 act(h, pd, scale=0.03125)
             else:
                 sc(h, pd, 0.03125, OP.mult)
+            if b == 0:
+                sc(B("offx"), B("sx2"), 448.0, OP.add)
         for b in range(4):
             o, w = B(xn, b, 4 * C, 4), I(B("yh%d" % b), B("offx"))
             if b % 2:

from concourse.mybir import dt, AluOpType, ActivationFunctionType

C, M, R, NS, MS = 448, 192, 3, 28, 12
MAGIC = 12582912.0
QN = [128, 128, 176, 240, 304, 368, 448]
BYSIGN = (24, 20, 19, 16, 12)
OP = AluOpType
AF = ActivationFunctionType

SCRATCH = {}
ALIAS = {}


def _sb(name, n, d):
    SCRATCH[name] = ("sbuf", [128, n], d)


def _mx(name, n):
    _sb("q" + name, n, "float8_e4m3fn_x4")
    _sb("s" + name, n, "uint8")


def _pack(buf, d, parts):
    at = 0
    for n, w in parts:
        ALIAS[n] = (buf, at, w)
        at += (w + 15) // 16 * 16
    _sb(buf, at, d)


def _packmx(buf, parts):
    at = 0
    for n, w in parts:
        ALIAS["q" + n] = ("q" + buf, at, w)
        ALIAS["s" + n] = ("s" + buf, at, w)
        at += w
    _mx(buf, at)


for _n in ("xa", "xb", "ft", "cr", "tl"):
    _sb(_n, 4 * C, "bfloat16")
_sb("ut", 512, "bfloat16")
_sb("vt", 512, "bfloat16")
_pack("kt", "bfloat16", [(n, 512) for n in ("ctile", "cneg", "fb", "sgt", "fst", "mst", "ont", "et0", "et1", "et2", "et3")])
_pack("tb", "bfloat16", [("t%d" % b, C) for b in range(4)])
_pack("yh", "bfloat16", [("yh%d" % b, C + M) for b in range(4)])
_pack("ctb", "bfloat16", [("ct%d" % q, 4 * QN[q]) for q in range(7)])
_pack("kb", "bfloat16", [("mk", C), ("rst", C), ("iotaj", C), ("mlt", M), ("kv", M), ("i16", C), ("jwm", C), ("jwf", C)])
_pack("sgn", "bfloat16", [("sgn%d" % k, 16 * k) for k in BYSIGN])
_packmx("k", [(n, 128) for n in ("e0", "e1", "e2", "e3", "sg", "fs", "ms", "on")])
_packmx("c", [("c%d" % q, QN[q]) for q in range(7)])
for _n, _w in (("u", 128), ("ux", 128), ("v", 128), ("w", 512), ("x", C), ("f", C), ("mv", 224), ("cr", C)):
    _mx(_n, _w)
for _t in range(R):
    _mx("tl%d" % _t, C)
    _mx("z%d" % _t, M)
    _mx("a%d" % _t, M)
for _n, _w in (("junk0", C), ("junk1", C), ("junk2", C), ("ot", C), ("la", C), ("lm", C), ("lf", C), ("ctab", C), ("cm", M), ("cf", M), ("lk", M), ("lkm", M),
               ("lkf", M), ("rep2", M), ("eqd", M), ("eqm", M), ("df", M), ("eqo", 12 * 192), ("st", C + M), ("stm", C), ("stf", C), ("rfb", C), ("em2", C),
               ("rf", C), ("dg", 112), ("mv", 896), ("m8", 112), ("lo", 112), ("hi", 112), ("gx", 56), ("gy", 56), ("gg", 224)):
    _sb(_n, _w, "bfloat16")
for _n in ("sm", "swf", "rep", "em", "ef", "iot512", "kca", "ka", "yo", "olf"):
    _sb(_n, C, "float32")
_pack("fk", "float32", [("cst", NS), ("onef", 32), ("gm", 8), ("mb", 32), ("rst8", 32), ("kc", NS), ("j448", NS), ("nt", MS)])
_pack("fw", "float32", [("rs", NS), ("rsc", NS), ("z", NS), ("x1", NS), ("kw", NS), ("km", 32), ("kf", 32), ("aa", 112), ("bb", 112), ("a2", 56), ("b2", 56),
                        ("av", NS), ("bv", NS), ("mn", NS), ("mxv", NS), ("spr", NS), ("sp5", NS), ("ab", NS), ("c1", NS), ("c2", NS), ("tg", NS),
                        ("dc", MS), ("dup", MS), ("dp1", MS), ("ntf", MS), ("lk2", MS), ("offf", MS), ("sx2", NS)])
_pack("ki", "int32", [("ia", C), ("ib", C), ("if1", NS), ("if2", 8)])
for _n, _w in (("offrep", NS), ("offu", 8), ("offq", NS), ("offt", NS), ("offs", NS), ("offr", NS), ("offc", MS), ("offl", NS), ("offd", MS), ("offx", NS)):
    _sb(_n, _w, "uint16")
for _n in ("pss", "psa", "psm", "psr", "pd0", "pd1", "pd2", "pd3"):
    SCRATCH[_n] = ("psum", [128, 512], "float32")

SEMAPHORES = ["sv", "ss", "sg", "st"] + ["arr%d" % t for t in range(R)] + ["snd%d" % t for t in range(R)] + ["d%d" % i for i in range(24)]


def make_queues(g, T):
    eng = {"v": g.vector, "s": g.scalar, "g": g, "t": g.tensor, "y": g.sync}
    sem = {"v": "sv", "s": "ss", "g": "sg", "t": "st"}
    count = {k: 0 for k in sem}
    known = {k: {} for k in eng}
    snap = {}
    log = {}
    ndma = [0]

    def psum(v):
        return SCRATCH[v[0]][0] == "psum"

    def region(v):
        return (0, 512, 1) if psum(v) else (v[1], v[2], v[3])

    def hit(p, q):
        if p[0] >= q[1] or q[0] >= p[1]:
            return False
        return not (p[2] == q[2] and p[2] > 1 and (p[0] - q[0]) % p[2])

    def wait(e, src, n):
        if known[e].get(src, 0) >= n:
            return
        eng[e].wait_ge(T.sem[sem.get(src, src)], n)
        known[e][src] = n
        for k, m in snap.get((src, n), {}).items():
            if known[e].get(k, 0) < m:
                known[e][k] = m

    def deps(e, outs, ins):
        need = {}
        for write, vs in ((True, outs), (False, ins)):
            for v in vs:
                r = region(v)
                for w2, r2, src, n in log.get(v[0], []):
                    if not hit(r, r2) or (e == "t" and src == "t"):
                        continue
                    if write or w2 or (psum(v) and src != e):
                        need[src] = max(need.get(src, 0), n)
        for src in sorted(need):
            wait(e, src, need[src])

    def record(outs, ins, src, n):
        for write, vs in ((True, outs), (False, ins)):
            for v in vs:
                r = region(v)
                L = log.setdefault(v[0], [])
                if write and not psum(v) and r[2] == 1:
                    L[:] = [x for x in L if not (r[0] <= x[1][0] and x[1][1] <= r[1])]
                L[:] = [x for x in L if not (x[0] == write and x[1] == r and x[2] == src)]
                L.append((write, r, src, n))

    def ap(v):
        x = T[v[0]][:, v[1]:v[2]:v[3]] if v[3] > 1 else T[v[0]][:, v[1]:v[2]]
        if len(v) > 4:
            if v[5] == "codes":
                x = x.bitcast(dt.uint32)
            if v[4] is not None:
                o = v[4]
                x = x.indirect(T[o[0]][:, o[1]:o[2]])
        return x

    def issue(e, outs, ins, call):
        deps(e, outs, ins)
        count[e] += 1
        call().then_inc(T.sem[sem[e]], 1)
        snap[(e, count[e])] = dict(known[e])
        record(outs, ins, e, count[e])

    def dma(e, out, in_, outs, ins, **kw):
        deps(e, outs, ins)
        name = "d%d" % ndma[0]
        ndma[0] += 1
        snap[(name, 16)] = dict(known[e])
        eng[e].dma_start(out, in_, **kw).then_inc(T.sem[name], 16)
        record(outs, ins, name, 16)

    def finish():
        for i in range(ndma[0]):
            wait("g", "d%d" % i, 16)
        for k in ("v", "s", "t", "g"):
            wait("g", k, count[k])

    return issue, dma, ap, wait, deps, finish


def rank_program(g, core, T, topo):
    rank = T.rank_of(core)
    if rank is None:
        return
    issue, dma, ap, wait, deps, finish = make_queues(g, T)

    def B(name, a=0, b=None, s=1):
        if name in ALIAS:
            buf, at, w = ALIAS[name]
        else:
            buf, at, w = name, 0, SCRATCH[name][1][1]
        return (buf, at + a, at + (w if b is None else b), s)

    def I(v, off, kind=""):
        return v + (off, kind)

    def srcs(*vs):
        r = []
        for v in vs:
            r.append(v)
            if len(v) > 4 and v[4] is not None:
                r.append(v[4])
        return r

    def tt(out, a, b, op):
        issue("v", [out], srcs(a, b), lambda: g.vector.tensor_tensor(ap(out), ap(a), ap(b), op))

    def sc(out, a, s1, op0, s2=None, op1=None):
        ins = srcs(a) + ([s1] if isinstance(s1, tuple) else [])
        x1 = ap(s1) if isinstance(s1, tuple) else s1
        if op1 is None:
            issue("v", [out], ins, lambda: g.vector.tensor_scalar(ap(out), ap(a), x1, None, op0))
        else:
            issue("v", [out], ins, lambda: g.vector.tensor_scalar(ap(out), ap(a), x1, s2, op0, op1))

    def scan(out, d0, d1, op0, op1):
        issue("v", [out], [d0, d1], lambda: g.vector.tensor_tensor_scan(ap(out), ap(d0), ap(d1), 0.0, op0, op1))

    def vcopy(out, a):
        ins = srcs(a) + ([out[4]] if len(out) > 4 and out[4] is not None else [])
        issue("v", [out], ins, lambda: g.vector.tensor_copy(ap(out), ap(a)))

    def act(out, a, func=AF.Copy, scale=None, bias=None, acc=None):
        kw = {}
        ins, outs = srcs(a), [out]
        for k, v in (("scale", scale), ("bias", bias)):
            if v is not None:
                kw[k] = ap(v) if isinstance(v, tuple) else v
                if isinstance(v, tuple):
                    ins.append(v)
        if acc is not None:
            kw["accum_out"] = ap(acc)
            outs.append(acc)
        issue("s", outs, ins, lambda: g.scalar.activation(ap(out), ap(a), func, **kw))

    nj = [0]

    def count_ones(acc, v, n):
        nj[0] = (nj[0] + 1) % 3
        act(B("junk%d" % nj[0], 0, n), v, acc=acc)

    def fill(v, c):
        issue("v", [v], [], lambda: g.vector.memset(ap(v), c))

    def quant(name, n, tile):
        src, o, s = B(tile, 0, 4 * n), B("q" + name, 0, n), B("s" + name, 0, n)
        issue("v", [o, s], [src], lambda: g.vector.quantize_mx(ap(o), ap(s), ap(src)))

    def mm(out, n, l, r, start=True, stop=True, la=0):
        o = B(out, 0, n)
        a, asc, b, bsc = B("q" + l, la, la + 128), B("s" + l, la, la + 128), B("q" + r, 0, n), B("s" + r, 0, n)
        issue("t", [o], [a, asc, b, bsc], lambda: g.tensor.matmul_mx(ap(o), ap(a), ap(asc), ap(b), ap(bsc), start, stop))

    def iota(v, pattern, base, cm):
        kw = {} if SCRATCH[v[0]][2] == "int32" else {"allow_small_or_imprecise_dtypes": True}
        issue("g", [v], [], lambda: g.iota(ap(v), pattern, base, cm, **kw))

    def sel(out, in_, pattern, op, base, cm):
        issue("g", [out], [in_], lambda: g.affine_select(ap(out), ap(in_), pattern, op, 0.0, base, cm))

    def last16(name, n=C):
        return B(name, 15, n, 16)

    def mask(out, v, n=C):
        scan(B(out, 0, n), v, B("mk", 0, n), OP.add, OP.mult)

    def hold(out, m, n=C):
        scan(B(out, 0, n), B("rst", 0, n), B(m, 0, n), OP.mult, OP.add)

    dma("y", T["xa"][:, :], T.x[:, :], [B("xa")], [])
    dma("s", T["ut"][:, :], T.u[:, :], [B("ut")], [])
    dma("y", T["qw"][:, 0:512].bitcast(dt.uint8), T.wc[:, :], [B("qw")], [])
    dma("s", T["sw"][:, :], T.ws[:, :], [B("sw")], [])
    dma("y", T["vt"][:, :], T.v[:, :], [B("vt")], [])

    def zeros(n):
        w = ALIAS[n][2]
        for a in range(0, w, 512):
            act(B(n, a, min(a + 512, w)), B("ctile", 0, min(512, w - a)), scale=0.0)

    iota(B("if2"), [[16, 8]], 0, 0)
    iota(B("ia"), [[0, NS], [-1, 16]], 1024, 1)
    iota(B("i16"), [[0, NS], [1, 16]], 0, 0)
    iota(B("if1"), [[16, NS]], 15, 0)
    fill(B("ctile"), 1.0)
    zeros("ct6")
    fill(B("ft"), 0.0)
    for a, b in (("ct4", "ct4"), ("ct3", "ct3"), ("ct0", "ct2")):
        n = ALIAS[b][1] + ALIAS[b][2] - ALIAS[a][1]
        o, i = B(a, 0, n), B("ft", 0, n)
        dma("y", ap(o), ap(i), [o], [i])
    fill(B("cneg"), -1.0)
    vcopy(B("offu"), B("if2"))
    fill(B("fst"), 0.0)
    sc(B("ib"), B("ia"), 15, OP.bitwise_and)
    sc(B("mk"), B("ib"), 0.0, OP.is_equal)
    sc(B("rst"), B("i16"), 1.0, OP.min)
    vcopy(B("offrep"), B("if1"))
    quant("u", 128, "ut")
    vcopy(I(B("qux"), None, "codes"), I(B("qu"), B("offu"), "codes"))
    act(B("sux"), I(B("su"), B("offu")))
    quant("x", C, "xa")
    zeros("ct5")

    sel(B("fb"), B("cneg"), [[-16, 8], [0, 16], [0, 4]], OP.is_ge, 0, 1)
    sel(B("sgt"), B("fb"), [[16, 8], [0, 16], [0, 4]], OP.is_ge, 15, -1)
    l0, l1, one = B("fst", 0, 512, 4), B("fst", 1, 512, 4), B("ctile", 0, 128)
    sel(l0, one, [[16, 8], [1, 16]], OP.is_gt, 0, -1)
    sel(l0, l0, [[-16, 8], [0, 16]], OP.is_ge, 0, 1)
    sel(l1, one, [[-16, 8], [-1, 16]], OP.is_gt, 0, 1)
    sel(l1, l1, [[16, 8], [0, 16]], OP.is_ge, 15, -1)
    iota(B("rs", 0, 1), [[0, 1]], 0, 0)
    iota(B("dc", 0, 1), [[0, 1]], 0, 0)
    iota(B("cst"), [[-16, NS]], 208, 0)
    iota(B("iotaj"), [[1, C]], -224, 0)
    iota(B("dg"), [[0, 112]], 0, 0)
    iota(B("onef"), [[0, 32]], 1, 0)
    sel(B("gm"), B("onef", 0, 8), [[-16, 8]], OP.is_ge, 0, 1)
    sel(B("gm"), B("gm"), [[16, 8]], OP.is_ge, 15, -1)
    sel(B("mb"), B("onef"), [[0, 4], [-16, 8]], OP.is_ge, 0, 1)
    sel(B("mb"), B("mb"), [[0, 4], [16, 8]], OP.is_ge, 15, -1)
    sel(B("rst8"), B("onef"), [[0, 4], [1, 8]], OP.is_gt, 0, 0)
    for b in range(4):
        sel(B("et%d" % b), B("ctile"), [[-4, 128], [-1, 4]], OP.is_equal, b, 4)
    sel(B("ont"), B("ctile"), [[0, 128], [-1000, 4]], OP.is_ge, 2936, 1)
    iota(B("iot512"), [[512, C]], 0, 0)
    iota(B("kca"), [[-1, C]], C - 1, 0)
    iota(B("kv"), [[1, M]], 0, 0)

    def consts_last():
        for e in range(4):
            act(B("mst", e, 512, 4), B("mk", 0, 128))
        mask("jwm", B("iotaj"))
        hold("jwf", "jwm")
        sc(B("j448"), last16("jwf"), -224.0, OP.add)
        sc(B("kc"), last16("jwf"), -1.0, OP.mult, 223.0, OP.add)
        sc(B("nt"), last16("jwf", M), 672.0, OP.add)
        quant("ms", 128, "mst")
        for b in range(4):
            quant("e%d" % b, 128, "et%d" % b)
        quant("on", 128, "ont")
        hold("jwm", "mk", M)
        sc(B("mlt"), B("jwm", 0, M), -1.0, OP.mult, 1.0, OP.add)
        quant("v", 128, "vt")

    X = ["xa", "xb"]
    for t in range(R):
        x, xn = X[t % 2], X[(t + 1) % 2]
        first = t == 0
        mm("pss", C, "ux", "x")
        mm("psm", C, "ux", "x")
        if not first:
            for b in range(4):
                mm("pd%d" % b, C, "e%d" % b, "x")
        tt(B("sm"), B("pss", 0, C), B("mk"), OP.mult)
        hold("swf", "sm")
        if not first:
            act(B("t0"), B("pd0", 0, C))

        def signs(q):
            for k in range(4 * q + 3, 4 * q - 1, -1):
                if k in BYSIGN:
                    act(B("sgn%d" % k), B("psm", 0, 16 * k), AF.Sign, scale=-1.0, bias=B("swf", 16 * k + 15, 16 * k + 16))

        signs(6)
        for q in (6, 5, 4, 3, 2, 1, 0):
            for k in range(4 * q + 3, max(4 * q - 1, 0), -1):
                c = B("ct%d" % q, k % 4, 64 * k, 4)
                if k in BYSIGN:
                    sc(c, B("sgn%d" % k), 0.0, OP.is_le)
                else:
                    sc(c, B("pss", 0, 16 * k), B("swf", 16 * k + 15, 16 * k + 16), OP.is_ge)
                if k == 4 * q + 3:
                    signs(q - 1)
                count_ones(B("rs", k, k + 1), c, 16 * k)
                if k == 23:
                    act(B("rep"), I(B("swf"), B("offrep")))
            if first and q == 6:
                quant("sg", 128, "sgt")
            quant("c%d" % q, QN[q], "ct%d" % q)
            mm("psa", QN[q], "sg", "c%d" % q, q == 6, q == 0)
            if q == 4:
                if first:
                    quant("fs", 128, "fst")
                tt(B("ft", 0, 4 * C, 4), B("pss", 0, C), B("rep"), OP.is_le)
                tt(B("ft", 1, 4 * C, 4), B("pss", 0, C), B("rep"), OP.is_lt)
                quant("f", C, "ft")
                mm("psa", C, "fs", "f", False, False)
            if q == 1 and first:
                consts_last()
        if first:
            for b in range(4):
                mm("pd%d" % b, C, "e%d" % b, "x")
            act(B("t0"), B("pd0", 0, C))
        act(B("t1"), B("pd1", 0, C))
        tt(B("em"), B("psa", 0, C), B("mk"), OP.mult)
        tt(B("rsc"), B("rs"), B("cst"), OP.add)
        hold("ef", "em")
        tt(B("z"), last16("ef"), B("rsc"), OP.add)
        sc(B("x1"), B("z"), 0.0625, OP.mult, MAGIC, OP.add)
        sc(B("offq"), B("z"), 224.0, OP.add)
        sc(B("dg", 0, 112, 4), B("x1"), -MAGIC, OP.add, 16.0, OP.mult)
        tt(B("dg", 1, 112, 4), B("z"), B("dg", 0, 112, 4), OP.subtract)
        for gr in range(4):
            act(B("mv", 112 * (gr + 4), 112 * (gr + 5)), B("dg"), scale=B("gm", gr + 4, gr + 5))
            sc(B("mv", 112 * gr, 112 * (gr + 1)), B("dg"), B("gm", gr, gr + 1), OP.mult)
        quant("mv", 224, "mv")
        mm("psm", 224, "ms", "mv")
        act(B("t2"), B("pd2", 0, C))
        act(B("t3"), B("pd3", 0, C))
        vcopy(I(B("ot"), B("offq")), B("iotaj"))
        vcopy(B("m8"), B("psm", 112, 224))
        tt(B("lo"), B("psm", 0, 112), B("m8"), OP.min)
        tt(B("hi"), B("psm", 0, 112), B("m8"), OP.max)
        tt(B("gg", 0, 56), B("lo", 0, 56), B("lo", 56, 112), OP.min)
        tt(B("gg", 168, 224), B("hi", 0, 56), B("hi", 56, 112), OP.max)
        tt(B("mn"), B("gg", 0, 28), B("gg", 28, 56), OP.min)
        tt(B("mxv"), B("gg", 168, 196), B("gg", 196, 224), OP.max)
        tt(B("gx"), B("lo", 0, 56), B("lo", 56, 112), OP.max)
        tt(B("spr"), B("mxv"), B("mn"), OP.subtract)
        tt(B("gy"), B("hi", 0, 56), B("hi", 56, 112), OP.min)
        sc(B("offs"), B("spr"), 0.0, OP.add)
        sc(B("sp5"), B("spr"), 512.0, OP.mult)
        tt(B("ka"), I(B("iot512"), B("offs")), B("kca"), OP.add)
        tt(B("kw"), B("sp5"), B("kc"), OP.add)
        tt(B("gg", 56, 112), B("gx"), B("gy"), OP.min)
        tt(B("km", 0, 24), B("kw", 0, 24), B("mb", 0, 24), OP.mult)
        tt(B("km", 24, 32), B("kw", 20, 28), B("mb", 24, 32), OP.mult)
        tt(B("gg", 112, 168), B("gx"), B("gy"), OP.max)
        scan(B("kf"), B("rst8"), B("km"), OP.mult, OP.add)
        for e in range(4):
            act(B("cr", e, 4 * C, 4), B("ka"), AF.Sign, scale=-1.0, bias=B("kf", 8 * e + 7, 8 * e + 8))
        for r in range(4):
            p, o = B("gg", 56 * r, 56 * r + 28), B("gg", 56 * (3 - r) + 28, 56 * (3 - r) + 56)
            tt(B("aa", 28 * r, 28 * r + 28), p, o, OP.min)
            tt(B("bb", 28 * r, 28 * r + 28), p, o, OP.max)
        tt(B("a2"), B("aa", 0, 56), B("aa", 56, 112), OP.max)
        tt(B("b2"), B("bb", 0, 56), B("bb", 56, 112), OP.min)
        tt(B("av"), B("a2", 0, 28), B("a2", 28, 56), OP.max)
        tt(B("bv"), B("b2", 0, 28), B("b2", 28, 56), OP.min)
        tt(B("c1"), B("z"), B("av"), OP.max)
        tt(B("ab"), B("av"), B("bv"), OP.add)
        tt(B("c2"), B("c1"), B("bv"), OP.min)
        tt(B("tg"), B("ab"), B("c2"), OP.subtract)
        sc(B("offt"), B("tg"), 224.0, OP.add)
        quant("cr", C, "cr")
        mm("psr", C, "on", "cr")
        act(B("rfb"), B("psr", 0, C), AF.Identity, scale=0.5, bias=-0.5)
        vcopy(B("la"), I(B("ot"), B("offt")))
        mask("lm", B("la"))
        hold("lf", "lm")
        mask("em2", B("rfb"))
        sc(B("offl"), last16("lf"), 224.0, OP.add)
        for b in range(4):
            act(B("tl", b, 4 * C, 4), I(B("t%d" % b), B("offl")))
        hold("rf", "em2")
        sc(B("offr"), last16("rf"), 224.0, OP.add)
        vcopy(I(B("ctab"), B("offr")), B("iotaj"))
        mask("cm", B("ctab", 0, M), M)
        hold("cf", "cm", M)
        sc(B("offc"), last16("cf", M), 224.0, OP.add)
        n_tl, n_z, n_a = "tl%d" % t, "z%d" % t, "a%d" % t
        act(B("lk"), I(B("la"), B("offc")))
        quant(n_tl, C, "tl")
        act(B("s" + n_z), I(B("s" + n_tl), B("offc")))
        vcopy(I(B("q" + n_z), None, "codes"), I(B("q" + n_tl), B("offc"), "codes"))
        to = T.cores[(rank + 1 + t) % len(T.cores)]
        rid, pid, _se = topo.addr(to)
        en = topo.engines(core, to)
        wide, thin = en[0::2], en[1::4]
        got = len(wide) + len(thin)
        for nm, view, es in (("s", lambda n: T["s" + n][:, 0:M], thin), ("q", lambda n: T["q" + n][:, 0:M].bitcast(dt.uint8), wide)):
            deps("g", [], [B(nm + n_z)])
            g.remote_dma(view(n_a), view(n_z), T.sem["arr%d" % t], T.sem["snd%d" % t], pid, rid, sum(1 << e for e in es))
        dma("g", T[x][:, :], T["tl"][:, :], [B(x)], [B("tl")], accum_op=OP.add)
        iota(B("st", 0, C), [[0, C]], -512, 0)
        mask("lkm", B("lk"), M)
        hold("lkf", "lkm", M)
        act(B("rep2"), I(B("lkf"), B("offrep", 0, MS)))
        for k in range(MS - 1, 0, -1):
            e = B("eqo", 192 * k, 192 * k + 16 * k)
            sc(e, B("lk", 0, 16 * k), B("lkf", 16 * k + 15, 16 * k + 16), OP.is_equal)
            count_ones(B("dc", k, k + 1), e, 16 * k)
        if t == R - 1:
            act(B("olf"), B("la"), AF.Identity, bias=224.0)
            dma("y", T.ol[:, :], T["olf"][0:128:16, :], [], [B("olf")])
        tt(B("eqd"), B("lk"), B("rep2"), OP.is_equal)
        scan(B("eqm"), B("eqd"), B("mlt"), OP.max, OP.mult)
        sc(B("lk2"), last16("lkf", M), 224.0, OP.add)
        scan(B("df"), B("rst", 0, M), B("eqm"), OP.mult, OP.max)
        tt(B("dup"), B("dc"), last16("df", M), OP.max)
        sc(B("dp1"), B("dup"), 1.0, OP.min)
        tt(B("ntf"), B("dp1"), B("nt"), OP.mult)
        tt(B("offf"), B("ntf"), B("lk2"), OP.max)
        sc(B("offd"), B("offf"), 0.0, OP.add)
        vcopy(I(B("st"), B("offd")), B("kv"))

        def halve(b):
            o, i = B("yh%d" % b, 0, C), B(x, b, 4 * C, 4)
            if b % 2:
                act(o, i, scale=0.5)
            else:
                sc(o, i, 0.5, OP.mult)

        halve(1)
        halve(3)
        mask("stm", B("st", 0, C))
        halve(0)
        hold("stf", "stm")
        halve(2)
        tt(B("sx2"), last16("stf"), B("j448"), OP.max)
        wait("t", "arr%d" % t, got)
        for b in range(4):
            mm("pd%d" % b, M, "w", n_a, la=128 * b)
        for b in range(4):
            h, pd = B("yh%d" % b, C, C + M), B("pd%d" % b, 0, M)
            if b % 2:
                act(h, pd, scale=0.03125)
            else:
                sc(h, pd, 0.03125, OP.mult)
            if b == 0:
                sc(B("offx"), B("sx2"), 448.0, OP.add)
        for b in range(4):
            o, w = B(xn, b, 4 * C, 4), I(B("yh%d" % b), B("offx"))
            if b % 2:
                act(o, w)
            else:
                vcopy(o, w)
        quant("x", C, xn)
    mm("pss", C, "v", "x")
    act(B("yo"), B("pss", 0, C))
    dma("y", T.oc[:, :], T["qx"][:, 0:C].bitcast(dt.uint8), [], [B("qx")])
    for k in range(4):
        dma("y", T.osc[4 * k:4 * k + 4, :], T["sx"][32 * k:32 * k + 4, 0:C], [], [B("sx")])
    dma("s", T.y[:, :], T["yo"][:, :], [], [B("yo")])
    for t in range(R):
        wait("g", "arr%d" % t, got)
        wait("g", "snd%d" % t, got)
    finish()
